import numpy as np
import ml_dtypes


def mxq(x, axis, fmt="e4m3"):
    dtype, down = {"e4m3": (ml_dtypes.float8_e4m3fn, 7), "e5m2": (ml_dtypes.float8_e5m2, 14)}[fmt]
    v = np.moveaxis(np.asarray(x, np.float32).astype(ml_dtypes.bfloat16).astype(np.float64), axis, -1)
    blocks = v.reshape(v.shape[:-1] + (-1, 32))
    amax = np.abs(blocks).max(-1, keepdims=True)
    byte = np.maximum(np.where(amax > 0, np.frexp(amax)[1] - 1 + 127, 0) - down, 1)
    scale = np.exp2(byte - 127.0)
    codes = (blocks / scale).astype(np.float32).astype(dtype).astype(np.float64)
    return np.moveaxis((codes * scale).reshape(v.shape), -1, axis)


WIDE = False


def mx_kscale(k):
    if not WIDE:
        return np.ones(k)
    levels = np.array([10, -10, 5, -5, 0])
    if k % 512:
        return np.exp2(np.random.permutation(np.resize(levels, k // 32))).repeat(32)
    a = np.empty((k // 512, 16))
    for p in range(k // 512):
        a[p, :8] = np.random.permutation(np.resize(levels, 8))
        for g in range(8):
            far = levels[np.abs(levels - a[p, g]) >= 10]
            a[p, g + 8] = far[np.random.randint(len(far))]
    return np.exp2(a.ravel()).repeat(32)


def f64(x):
    return np.asarray(x).astype(np.float64)


def striped(idx):
    return np.tile(idx.reshape(-1, 16).T, (8, 1)).astype(np.uint16)


def unstriped(offs):
    return offs[:16].T.reshape(-1).astype(np.int64)


def relu(v):
    return np.maximum(v, 0.0)


K, T, E, C, H, N = 1024, 512, 4, 256, 512, 128


def by_expert(wq, xq):
    return np.concatenate([wq[e].T @ xq[:, e * C:(e + 1) * C] for e in range(E)], axis=1)


def setup_inputs():
    n = np.random.standard_normal
    s = mx_kscale(K)[:, None]
    u = mx_kscale(H)
    first = np.random.permutation(np.repeat(np.arange(E), T // E))
    second = (first + 1 + np.random.permutation(np.repeat(np.arange(E - 1), -(-T // (E - 1)))[:T])) % E
    while np.bincount(second, minlength=E).max() != T // E:
        load = np.bincount(second, minlength=E); hi, lo = int(load.argmax()), int(load.argmin())
        t = np.flatnonzero((second == hi) & (first != lo))[0]; second[t] = lo
    slot_token = np.empty(E * C, np.int64); pos = np.empty((2, T), np.int64); fill = np.zeros(E, np.int64)
    place = np.stack([np.random.permutation(C) for _ in range(E)])
    for r, deal in enumerate((first, second)):
        for t in np.random.permutation(T):
            e = deal[t]; j = e * C + place[e, fill[e]]; fill[e] += 1; slot_token[j] = t; pos[r, t] = j
    g = np.random.uniform(0.2, 0.8, T)
    return {
        "xT": (n((K, T)) * s).astype(np.float32),
        "w1": (n((E, K, H)) / np.sqrt(K) / s[None] * u[None, None, :]).astype(np.float32),
        "w2": (n((E, H, N)) / np.sqrt(H) / u[None, :, None]).astype(np.float32),
        "gate": np.stack([np.tile(g, (N, 1)), np.tile(1.0 - g, (N, 1))]).astype(np.float32),
        "offs": striped(slot_token),
        "pos1": striped(pos[0]),
        "pos2": striped(pos[1]),
    }


def reference(xT, w1, w2, gate, offs, pos1, pos2):
    idx = unstriped(offs)
    xq = mxq(f64(xT)[:, idx], 0, "e4m3")
    h = relu(by_expert(mxq(f64(w1), 1, "e4m3"), xq))
    y = by_expert(mxq(f64(w2), 1, "e4m3"), mxq(h, 0, "e4m3"))
    return f64(gate[0]) * y[:, unstriped(pos1)] + f64(gate[1]) * y[:, unstriped(pos2)]

@@ -1,0 +1,181 @@
+from contextlib import ExitStack
+
+import concourse.mybir as mybir
+
+F32 = mybir.dt.float32
+BF16 = mybir.dt.bfloat16
+U32 = mybir.dt.uint32
+U16 = mybir.dt.uint16
+U8 = mybir.dt.uint8
+FP8X4 = mybir.dt.float8_e4m3fn_x4
+MULT = mybir.AluOpType.mult
+ADD = mybir.AluOpType.add
+RELU = mybir.ActivationFunctionType.Relu
+
+K, T, E, C, H, N = 1024, 512, 4, 256, 512, 128
+P = 128
+PASSES = K // 512
+SLOTS = E * C
+CHUNK = 128
+
+FLOPS = 2 * SLOTS * (K * H + H * N)
+
+CUTS = [(0, 384), (384, 768), (768, 1024)]
+
+
+def tile_routed_moe_kernel(tc, xT, w1, w2, gate, offs, pos1, pos2, out):
+    nc = tc.nc
+    with ExitStack() as ctx:
+        lists = ctx.enter_context(tc.tile_pool(name="lists", bufs=1))
+        keep = ctx.enter_context(tc.tile_pool(name="keep", bufs=1))
+        sums = ctx.enter_context(tc.psum_pool(name="sums", bufs=5))
+        ysums = ctx.enter_context(tc.psum_pool(name="ysums", bufs=3))
+
+        offs_sb = lists.tile([P, SLOTS // 16], U16, name="offs_sb")
+        pos1_sb = lists.tile([P, T // 16], U16, name="pos1_sb")
+        pos2_sb = lists.tile([P, T // 16], U16, name="pos2_sb")
+
+        x_raw = []
+        for a in range(PASSES):
+            raw = keep.tile([P, 4, T], F32, name="x_raw%d" % a)
+            nc.sync.dma_start(out=raw[:], in_=xT[512 * a : 512 * (a + 1), :].rearrange("(p j) t -> p j t", j=4))
+            x_raw.append(raw)
+            if a == 0:
+                nc.sync.dma_start(offs_sb[:], offs)
+        w1_raw = {}
+        for e in range(E):
+            for a in range(PASSES):
+                raw = keep.tile([P, 4, H], F32, name="w1_raw%d%d" % (e, a))
+                nc.sync.dma_start(out=raw[:], in_=w1[e, 512 * a : 512 * (a + 1), :].rearrange("(p j) h -> p j h", j=4))
+                w1_raw[e, a] = raw
+        w2_raw = keep.tile([P, E, 4, N], F32, name="w2_raw")
+        nc.sync.dma_start(
+            out=w2_raw[:].rearrange("p e j n -> p e (j n)"),
+            in_=w2.rearrange("e (p j) n -> p e (j n)", j=4),
+        )
+        nc.sync.dma_start(pos1_sb[:], pos1)
+        nc.sync.dma_start(pos2_sb[:], pos2)
+        gate_sb = keep.tile([P, 2, T], F32, name="gate_sb")
+        nc.sync.dma_start(out=gate_sb[:], in_=gate.rearrange("r p t -> p r t"))
+
+        g_words = []
+        g_bytes = []
+        x_bytes = []
+        for a in range(PASSES):
+            by = keep.tile([P, T], U8, name="x_bytes%d" % a, align_bytes=64)
+            nc.gpsimd.memset(by[:], 0)
+            x_bytes.append(by)
+        for a in range(PASSES):
+            grouped = keep.tile([P, T, 4], BF16, name="x_grouped%d" % a, align_bytes=64)
+            dst = grouped[:].rearrange("p (c i) j -> p c j i", i=4)
+            src = x_raw[a][:].rearrange("p j (c i) -> p c j i", i=4)
+            cut = 88 if a == 0 else 32
+            nc.vector.tensor_copy(out=dst[:, :cut], in_=src[:, :cut])
+            nc.scalar.copy(out=dst[:, cut:], in_=src[:, cut:])
+            words = keep.tile([P, T], U32, name="x_words%d" % a, align_bytes=64)
+            nc.vector.quantize_mx(
+                out=words[:].bitcast(FP8X4), scales=x_bytes[a][:], in_=grouped[:].rearrange("p t j -> p (t j)")
+            )
+            gw = keep.tile([P, SLOTS], U32, name="g_words%d" % a, align_bytes=64)
+            gb = keep.tile([P, SLOTS], U8, name="g_bytes%d" % a, align_bytes=64)
+            for lo, hi in CUTS:
+                sel = offs_sb[:, lo // 16 : hi // 16]
+                nc.vector.tensor_copy(out=gw[:, lo:hi], in_=words[:].indirect(sel))
+                nc.vector.tensor_copy(out=gb[:, lo:hi], in_=x_bytes[a][:].indirect(sel))
+            g_words.append(gw)
+            g_bytes.append(gb)
+
+        w1_codes = {}
+        w1_scales = {}
+
+        def copy_w1(e, a, cut):
+            grouped = keep.tile([P, 4 * H], BF16, name="w1_grouped%d%d" % (e, a), tag="grouped%d%d" % (e, a), align_bytes=64)
+            dst = grouped[:].rearrange("p (t m j) -> p m j t", t=4, j=4)
+            src = w1_raw[e, a][:].rearrange("p j (m t) -> p m j t", t=4)
+            if cut > 0:
+                nc.vector.tensor_copy(out=dst[:, :cut], in_=src[:, :cut])
+            if cut < 128:
+                nc.scalar.copy(out=dst[:, cut:], in_=src[:, cut:])
+            return grouped
+
+        def quantise_w1(e, a, grouped):
+            codes = keep.tile([P, H], U32, name="w1_codes%d%d" % (e, a), align_bytes=64)
+            scales = keep.tile([P, H], U8, name="w1_scales%d%d" % (e, a), align_bytes=64)
+            nc.vector.quantize_mx(out=codes[:].bitcast(FP8X4), scales=scales[:], in_=grouped[:])
+            w1_codes[e, a] = codes
+            w1_scales[e, a] = scales
+
+        VECTOR_SHARE = {(3, 0): 64, (3, 1): 64}
+        for e in range(E):
+            for a in range(PASSES):
+                quantise_w1(e, a, copy_w1(e, a, VECTOR_SHARE.get((e, a), 0)))
+
+        w2_grouped = keep.tile([P, E, N, 4], BF16, name="w2_grouped", align_bytes=64)
+        nc.vector.tensor_copy(
+            out=w2_grouped[:].rearrange("p e (c i) j -> p e c j i", i=4),
+            in_=w2_raw[:].rearrange("p e j (c i) -> p e c j i", i=4),
+        )
+        w2_codes = keep.tile([P, E, N], U32, name="w2_codes", align_bytes=64)
+        w2_scales = keep.tile([P, E, N], U8, name="w2_scales", align_bytes=64)
+        nc.vector.quantize_mx(
+            out=w2_codes[:].rearrange("p e n -> p (e n)").bitcast(FP8X4),
+            scales=w2_scales[:].rearrange("p e n -> p (e n)"),
+            in_=w2_grouped[:].rearrange("p e n j -> p (e n j)"),
+        )
+
+        y_sb = keep.tile([P, SLOTS], F32, name="y_sb")
+        H_TAGS = ["grouped20", "grouped21", "h2", "h3"]
+        h_grouped = [
+            keep.tile([P, C, 4], BF16, name="h_grouped%d" % e, tag=H_TAGS[e], align_bytes=64) for e in range(E)
+        ]
+        h_codes = [keep.tile([P, C], U32, name="h_codes%d" % e, align_bytes=64) for e in range(E)]
+        h_scales = [keep.tile([P, C], U8, name="h_scales%d" % e, align_bytes=64) for e in range(E)]
+        for e in range(E):
+            for c in range(C // CHUNK):
+                slots = slice(e * C + c * CHUNK, e * C + (c + 1) * CHUNK)
+                acc = sums.tile([P, 4, CHUNK], F32, name="acc")
+                for t in range(4):
+                    for a in range(PASSES):
+                        nc.tensor.matmul_mx(
+                            out=acc[:, t, :],
+                            lhsT=w1_codes[e, a][:, t * P : (t + 1) * P].bitcast(FP8X4),
+                            lhsT_scale=w1_scales[e, a][:, t * P : (t + 1) * P],
+                            rhs=g_words[a][:, slots].bitcast(FP8X4),
+                            rhs_scale=g_bytes[a][:, slots],
+                            start=(a == 0),
+                            stop=(a == PASSES - 1),
+                        )
+                h_out = h_grouped[e][:, c * CHUNK : (c + 1) * CHUNK, :]
+                h_in = acc[:].rearrange("p t n -> p n t")
+                if e == E - 1 and c == 1:
+                    nc.vector.tensor_scalar_max(out=h_out, in0=h_in, scalar1=0.0)
+                else:
+                    nc.scalar.activation(out=h_out, in_=h_in, func=RELU)
+            parts = 2 if e == E - 1 else 1
+            w = C // parts
+            for c in range(parts):
+                nc.vector.quantize_mx(
+                    out=h_codes[e][:, c * w : (c + 1) * w].bitcast(FP8X4),
+                    scales=h_scales[e][:, c * w : (c + 1) * w],
+                    in_=h_grouped[e][:, c * w : (c + 1) * w, :].rearrange("p n t -> p (n t)"),
+                )
+        for e in range(E):
+            ysum = ysums.tile([P, C], F32, name="ysum")
+            nc.tensor.matmul_mx(
+                out=ysum[:],
+                lhsT=w2_codes[:, e, :].bitcast(FP8X4),
+                lhsT_scale=w2_scales[:, e, :],
+                rhs=h_codes[e][:].bitcast(FP8X4),
+                rhs_scale=h_scales[e][:],
+                start=True,
+                stop=True,
+            )
+            nc.scalar.copy(out=y_sb[:, e * C : (e + 1) * C], in_=ysum[:])
+
+        p1 = keep.tile([P, T], F32, name="p1")
+        p2 = keep.tile([P, T], F32, name="p2")
+        res = keep.tile([P, T], F32, name="res")
+        nc.vector.tensor_tensor(out=p1[:], in0=y_sb[:].indirect(pos1_sb[:]), in1=gate_sb[:, 0, :], op=MULT)
+        nc.vector.tensor_tensor(out=p2[:], in0=y_sb[:].indirect(pos2_sb[:]), in1=gate_sb[:, 1, :], op=MULT)
+        nc.vector.tensor_tensor(out=res[:], in0=p1[:], in1=p2[:], op=ADD)
+        nc.sync.dma_start(out=out, in_=res[:])

@@ -43,8 +43,9 @@ def tile_routed_moe_kernel(tc, xT, w1, w2, gate, offs, pos1, pos2, out):
             if a == 0:
                 nc.sync.dma_start(offs_sb[:], offs)
         w1_raw = {}
-        for e in range(E):
-            for a in range(PASSES):
+        LOAD_ORDER = [(0, 0), (0, 1), (1, 0), (1, 1), (2, 0), (2, 1), (3, 0), (3, 1)]
+        for e, a in LOAD_ORDER:
+            if True:
                 raw = keep.tile([P, 4, H], F32, name="w1_raw%d%d" % (e, a))
                 nc.sync.dma_start(out=raw[:], in_=w1[e, 512 * a : 512 * (a + 1), :].rearrange("(p j) h -> p j h", j=4))
                 w1_raw[e, a] = raw
@@ -69,9 +70,15 @@ def tile_routed_moe_kernel(tc, xT, w1, w2, gate, offs, pos1, pos2, out):
             grouped = keep.tile([P, T, 4], BF16, name="x_grouped%d" % a, align_bytes=64)
             dst = grouped[:].rearrange("p (c i) j -> p c j i", i=4)
             src = x_raw[a][:].rearrange("p j (c i) -> p c j i", i=4)
-            cut = 88 if a == 0 else 32
-            nc.vector.tensor_copy(out=dst[:, :cut], in_=src[:, :cut])
-            nc.scalar.copy(out=dst[:, cut:], in_=src[:, cut:])
+            vcut, gcut = ((52, 88), (0, 0))[a]
+            if vcut > 0:
+                nc.vector.tensor_copy(out=dst[:, :vcut], in_=src[:, :vcut])
+            if gcut > vcut:
+                nc.gpsimd.tensor_copy(
+                    out=grouped[:, 4 * vcut : 4 * gcut, :],
+                    in_=x_raw[a][:, :, 4 * vcut : 4 * gcut].rearrange("p j t -> p t j"),
+                )
+            nc.scalar.copy(out=dst[:, gcut:], in_=src[:, gcut:])
             words = keep.tile([P, T], U32, name="x_words%d" % a, align_bytes=64)
             nc.vector.quantize_mx(
                 out=words[:].bitcast(FP8X4), scales=x_bytes[a][:], in_=grouped[:].rearrange("p t j -> p (t j)")
@@ -88,14 +95,19 @@ def tile_routed_moe_kernel(tc, xT, w1, w2, gate, offs, pos1, pos2, out):
         w1_codes = {}
         w1_scales = {}
 
-        def copy_w1(e, a, cut):
+        def copy_w1(e, a, cut, gcut):
             grouped = keep.tile([P, 4 * H], BF16, name="w1_grouped%d%d" % (e, a), tag="grouped%d%d" % (e, a), align_bytes=64)
             dst = grouped[:].rearrange("p (t m j) -> p m j t", t=4, j=4)
             src = w1_raw[e, a][:].rearrange("p j (m t) -> p m j t", t=4)
             if cut > 0:
                 nc.vector.tensor_copy(out=dst[:, :cut], in_=src[:, :cut])
-            if cut < 128:
-                nc.scalar.copy(out=dst[:, cut:], in_=src[:, cut:])
+            for m in range(cut, gcut, 128):
+                nc.gpsimd.tensor_copy(
+                    out=grouped[:].rearrange("p (t m j) -> p t m j", t=4, j=4)[:, :, m:gcut],
+                    in_=w1_raw[e, a][:].rearrange("p j (m t) -> p t m j", t=4)[:, :, m:gcut],
+                )
+            if gcut < 128:
+                nc.scalar.copy(out=dst[:, gcut:], in_=src[:, gcut:])
             return grouped
 
         def quantise_w1(e, a, grouped):
@@ -105,32 +117,32 @@ def tile_routed_moe_kernel(tc, xT, w1, w2, gate, offs, pos1, pos2, out):
             w1_codes[e, a] = codes
             w1_scales[e, a] = scales
 
-        VECTOR_SHARE = {(3, 0): 64, (3, 1): 64}
-        for e in range(E):
-            for a in range(PASSES):
-                quantise_w1(e, a, copy_w1(e, a, VECTOR_SHARE.get((e, a), 0)))
+        SHARES = {(0, 0): (0, 64), (0, 1): (0, 64), (1, 0): (0, 64), (1, 1): (0, 64), (2, 0): (0, 48), (2, 1): (64, 64), (3, 0): (64, 64), (3, 1): (128, 128)}
+        def prepare_w1(e, a):
+            quantise_w1(e, a, copy_w1(e, a, *SHARES.get((e, a), (0, 0))))
 
-        w2_grouped = keep.tile([P, E, N, 4], BF16, name="w2_grouped", align_bytes=64)
-        nc.vector.tensor_copy(
-            out=w2_grouped[:].rearrange("p e (c i) j -> p e c j i", i=4),
-            in_=w2_raw[:].rearrange("p e j (c i) -> p e c j i", i=4),
-        )
-        w2_codes = keep.tile([P, E, N], U32, name="w2_codes", align_bytes=64)
-        w2_scales = keep.tile([P, E, N], U8, name="w2_scales", align_bytes=64)
-        nc.vector.quantize_mx(
-            out=w2_codes[:].rearrange("p e n -> p (e n)").bitcast(FP8X4),
-            scales=w2_scales[:].rearrange("p e n -> p (e n)"),
-            in_=w2_grouped[:].rearrange("p e n j -> p (e n j)"),
-        )
+        def prepare_w2():
+            w2_grouped = keep.tile([P, E, N, 4], BF16, name="w2_grouped", align_bytes=64)
+            nc.vector.tensor_copy(
+                out=w2_grouped[:].rearrange("p e (c i) j -> p e c j i", i=4),
+                in_=w2_raw[:].rearrange("p e j (c i) -> p e c j i", i=4),
+            )
+            w2_codes = keep.tile([P, E, N], U32, name="w2_codes", align_bytes=64)
+            w2_scales = keep.tile([P, E, N], U8, name="w2_scales", align_bytes=64)
+            nc.vector.quantize_mx(
+                out=w2_codes[:].rearrange("p e n -> p (e n)").bitcast(FP8X4),
+                scales=w2_scales[:].rearrange("p e n -> p (e n)"),
+                in_=w2_grouped[:].rearrange("p e n j -> p (e n j)"),
+            )
+            return w2_codes, w2_scales
 
         y_sb = keep.tile([P, SLOTS], F32, name="y_sb")
-        H_TAGS = ["grouped20", "grouped21", "h2", "h3"]
-        h_grouped = [
-            keep.tile([P, C, 4], BF16, name="h_grouped%d" % e, tag=H_TAGS[e], align_bytes=64) for e in range(E)
-        ]
+        H_TAGS = ["grouped21", "grouped30", "h2", "h3"]
+        h_grouped = {}
         h_codes = [keep.tile([P, C], U32, name="h_codes%d" % e, align_bytes=64) for e in range(E)]
         h_scales = [keep.tile([P, C], U8, name="h_scales%d" % e, align_bytes=64) for e in range(E)]
-        for e in range(E):
+        def layer1(e):
+            h_grouped[e] = keep.tile([P, C, 4], BF16, name="h_grouped%d" % e, tag=H_TAGS[e], align_bytes=64)
             for c in range(C // CHUNK):
                 slots = slice(e * C + c * CHUNK, e * C + (c + 1) * CHUNK)
                 acc = sums.tile([P, 4, CHUNK], F32, name="acc")
@@ -147,10 +159,7 @@ def tile_routed_moe_kernel(tc, xT, w1, w2, gate, offs, pos1, pos2, out):
                         )
                 h_out = h_grouped[e][:, c * CHUNK : (c + 1) * CHUNK, :]
                 h_in = acc[:].rearrange("p t n -> p n t")
-                if e == E - 1 and c == 1:
-                    nc.vector.tensor_scalar_max(out=h_out, in0=h_in, scalar1=0.0)
-                else:
-                    nc.scalar.activation(out=h_out, in_=h_in, func=RELU)
+                nc.scalar.activation(out=h_out, in_=h_in, func=RELU)
             parts = 2 if e == E - 1 else 1
             w = C // parts
             for c in range(parts):
@@ -159,6 +168,17 @@ def tile_routed_moe_kernel(tc, xT, w1, w2, gate, offs, pos1, pos2, out):
                     scales=h_scales[e][:, c * w : (c + 1) * w],
                     in_=h_grouped[e][:, c * w : (c + 1) * w, :].rearrange("p n t -> p (n t)"),
                 )
+        for e in range(3):
+            for a in range(PASSES):
+                prepare_w1(e, a)
+        layer1(0)
+        prepare_w1(3, 0)
+        layer1(1)
+        prepare_w1(3, 1)
+        layer1(2)
+        layer1(3)
+        w2_codes, w2_scales = prepare_w2()
+
         for e in range(E):
             ysum = ysums.tile([P, C], F32, name="ysum")
             nc.tensor.matmul_mx(

@@ -14,13 +14,22 @@ RELU = mybir.ActivationFunctionType.Relu
 
 K, T, E, C, H, N = 1024, 512, 4, 256, 512, 128
 P = 128
-PASSES = K // 512
+PACK = 4
+PASS = P * PACK
+PASSES = K // PASS
 SLOTS = E * C
 CHUNK = 128
+LIST_ROWS = 16
 
 FLOPS = 2 * SLOTS * (K * H + H * N)
 
-CUTS = [(0, 384), (384, 768), (768, 1024)]
+GATHER_CUTS = [(0, 384), (384, 768), (768, 1024)]
+
+X_VECTOR_GROUPS = (88, 16)
+W1_VECTOR_GROUPS = {(1, 0): 128, (2, 1): 128, (3, 0): 16, (3, 1): 48}
+
+H_BF16_AFTER = {0: "w1_raw20", 1: "w1_raw31", 2: "w1_bf16_30"}
+H_CODES_AFTER = {0: "w1_bf16_11", 1: "w1_bf16_20", 2: "w1_raw21"}
 
 
 def tile_routed_moe_kernel(tc, xT, w1, w2, gate, offs, pos1, pos2, out):
@@ -28,174 +37,147 @@ def tile_routed_moe_kernel(tc, xT, w1, w2, gate, offs, pos1, pos2, out):
     with ExitStack() as ctx:
         lists = ctx.enter_context(tc.tile_pool(name="lists", bufs=1))
         keep = ctx.enter_context(tc.tile_pool(name="keep", bufs=1))
-        sums = ctx.enter_context(tc.psum_pool(name="sums", bufs=5))
-        ysums = ctx.enter_context(tc.psum_pool(name="ysums", bufs=3))
+        hidden_banks = ctx.enter_context(tc.psum_pool(name="hidden_banks", bufs=4))
+        y_banks = ctx.enter_context(tc.psum_pool(name="y_banks", bufs=1))
 
-        offs_sb = lists.tile([P, SLOTS // 16], U16, name="offs_sb")
-        pos1_sb = lists.tile([P, T // 16], U16, name="pos1_sb")
-        pos2_sb = lists.tile([P, T // 16], U16, name="pos2_sb")
+        def aligned(shape, dtype, name, tag=None):
+            return keep.tile(shape, dtype, name=name, tag=tag or name, align_bytes=64)
 
-        x_raw = []
+        def quantise(codes, scales, grouped):
+            nc.vector.quantize_mx(out=codes.bitcast(FP8X4), scales=scales, in_=grouped)
+
+        offs_sb = lists.tile([P, SLOTS // LIST_ROWS], U16, name="offs_sb")
+        pos1_sb = lists.tile([P, T // LIST_ROWS], U16, name="pos1_sb")
+        pos2_sb = lists.tile([P, T // LIST_ROWS], U16, name="pos2_sb")
+        x_raw = [aligned([P, PACK, T], F32, "x_raw%d" % a) for a in range(PASSES)]
+        w1_raw = {}
         for a in range(PASSES):
-            raw = keep.tile([P, 4, T], F32, name="x_raw%d" % a)
-            nc.sync.dma_start(out=raw[:], in_=xT[512 * a : 512 * (a + 1), :].rearrange("(p j) t -> p j t", j=4))
-            x_raw.append(raw)
+            rows = xT[PASS * a : PASS * (a + 1), :]
+            nc.sync.dma_start(out=x_raw[a][:], in_=rows.rearrange("(p j) t -> p j t", j=PACK))
             if a == 0:
                 nc.sync.dma_start(offs_sb[:], offs)
-        w1_raw = {}
-        LOAD_ORDER = [(0, 0), (0, 1), (1, 0), (1, 1), (2, 0), (2, 1), (3, 0), (3, 1)]
-        for e, a in LOAD_ORDER:
-            if True:
-                raw = keep.tile([P, 4, H], F32, name="w1_raw%d%d" % (e, a))
-                nc.sync.dma_start(out=raw[:], in_=w1[e, 512 * a : 512 * (a + 1), :].rearrange("(p j) h -> p j h", j=4))
-                w1_raw[e, a] = raw
-        w2_raw = keep.tile([P, E, 4, N], F32, name="w2_raw")
+        for e in range(E):
+            for a in range(PASSES):
+                w1_raw[e, a] = aligned([P, PACK, H], F32, "w1_raw%d%d" % (e, a))
+                rows = w1[e, PASS * a : PASS * (a + 1), :]
+                nc.sync.dma_start(out=w1_raw[e, a][:], in_=rows.rearrange("(p j) i -> p j i", j=PACK))
+        w2_raw = aligned([P, E, PACK, N], F32, "w2_raw")
         nc.sync.dma_start(
             out=w2_raw[:].rearrange("p e j n -> p e (j n)"),
-            in_=w2.rearrange("e (p j) n -> p e (j n)", j=4),
+            in_=w2.rearrange("e (p j) n -> p e (j n)", j=PACK),
         )
         nc.sync.dma_start(pos1_sb[:], pos1)
         nc.sync.dma_start(pos2_sb[:], pos2)
         gate_sb = keep.tile([P, 2, T], F32, name="gate_sb")
-        nc.sync.dma_start(out=gate_sb[:], in_=gate.rearrange("r p t -> p r t"))
+        nc.sync.dma_start(out=gate_sb[:], in_=gate.rearrange("r n t -> n r t"))
 
-        g_words = []
-        g_bytes = []
-        x_bytes = []
+        x_bytes = aligned([P, T], U8, "x_bytes")
+        nc.gpsimd.memset(x_bytes[:], 0)
+        slot_words = [aligned([P, SLOTS], U32, "slot_words%d" % a) for a in range(PASSES)]
+        slot_bytes = aligned([P, SLOTS], U8, "slot_bytes")
         for a in range(PASSES):
-            by = keep.tile([P, T], U8, name="x_bytes%d" % a, align_bytes=64)
-            nc.gpsimd.memset(by[:], 0)
-            x_bytes.append(by)
-        for a in range(PASSES):
-            grouped = keep.tile([P, T, 4], BF16, name="x_grouped%d" % a, align_bytes=64)
-            dst = grouped[:].rearrange("p (c i) j -> p c j i", i=4)
+            x_bf16 = aligned([P, T, PACK], BF16, "x_bf16_%d" % a)
+            dst = x_bf16[:].rearrange("p (c i) j -> p c j i", i=4)
             src = x_raw[a][:].rearrange("p j (c i) -> p c j i", i=4)
-            vcut, gcut = ((52, 88), (0, 0))[a]
-            if vcut > 0:
-                nc.vector.tensor_copy(out=dst[:, :vcut], in_=src[:, :vcut])
-            if gcut > vcut:
-                nc.gpsimd.tensor_copy(
-                    out=grouped[:, 4 * vcut : 4 * gcut, :],
-                    in_=x_raw[a][:, :, 4 * vcut : 4 * gcut].rearrange("p j t -> p t j"),
-                )
-            nc.scalar.copy(out=dst[:, gcut:], in_=src[:, gcut:])
-            words = keep.tile([P, T], U32, name="x_words%d" % a, align_bytes=64)
-            nc.vector.quantize_mx(
-                out=words[:].bitcast(FP8X4), scales=x_bytes[a][:], in_=grouped[:].rearrange("p t j -> p (t j)")
-            )
-            gw = keep.tile([P, SLOTS], U32, name="g_words%d" % a, align_bytes=64)
-            gb = keep.tile([P, SLOTS], U8, name="g_bytes%d" % a, align_bytes=64)
-            for lo, hi in CUTS:
-                sel = offs_sb[:, lo // 16 : hi // 16]
-                nc.vector.tensor_copy(out=gw[:, lo:hi], in_=words[:].indirect(sel))
-                nc.vector.tensor_copy(out=gb[:, lo:hi], in_=x_bytes[a][:].indirect(sel))
-            g_words.append(gw)
-            g_bytes.append(gb)
+            cut = X_VECTOR_GROUPS[a]
+            nc.vector.tensor_copy(out=dst[:, :cut], in_=src[:, :cut])
+            nc.scalar.copy(out=dst[:, cut:], in_=src[:, cut:])
+            x_words = aligned([P, T], U32, "x_words%d" % a)
+            quantise(x_words[:], x_bytes[4 * a :, :], x_bf16[:].rearrange("p t j -> p (t j)"))
+            for lo, hi in GATHER_CUTS:
+                token_of_slot = offs_sb[:, lo // LIST_ROWS : hi // LIST_ROWS]
+                nc.vector.tensor_copy(out=slot_words[a][:, lo:hi], in_=x_words[:].indirect(token_of_slot))
+        for lo, hi in GATHER_CUTS:
+            token_of_slot = offs_sb[:, lo // LIST_ROWS : hi // LIST_ROWS]
+            nc.vector.tensor_copy(out=slot_bytes[:, lo:hi], in_=x_bytes[:].indirect(token_of_slot))
 
         w1_codes = {}
         w1_scales = {}
+        for e in range(E):
+            for a in range(PASSES):
+                w1_bf16 = aligned([P, PACK * H], BF16, "w1_bf16_%d%d" % (e, a))
+                dst = w1_bf16[:].rearrange("p (t m j) -> p m j t", t=4, j=PACK)
+                src = w1_raw[e, a][:].rearrange("p j (m t) -> p m j t", t=4)
+                cut = W1_VECTOR_GROUPS.get((e, a), 0)
+                if cut > 0:
+                    nc.vector.tensor_copy(out=dst[:, :cut], in_=src[:, :cut])
+                if cut < H // 4:
+                    nc.scalar.copy(out=dst[:, cut:], in_=src[:, cut:])
+                w1_codes[e, a] = aligned([P, H], U32, "w1_codes%d%d" % (e, a))
+                w1_scales[e, a] = aligned([P, H], U8, "w1_scales%d%d" % (e, a))
+                quantise(w1_codes[e, a][:], w1_scales[e, a][:], w1_bf16[:])
 
-        def copy_w1(e, a, cut, gcut):
-            grouped = keep.tile([P, 4 * H], BF16, name="w1_grouped%d%d" % (e, a), tag="grouped%d%d" % (e, a), align_bytes=64)
-            dst = grouped[:].rearrange("p (t m j) -> p m j t", t=4, j=4)
-            src = w1_raw[e, a][:].rearrange("p j (m t) -> p m j t", t=4)
-            if cut > 0:
-                nc.vector.tensor_copy(out=dst[:, :cut], in_=src[:, :cut])
-            for m in range(cut, gcut, 128):
-                nc.gpsimd.tensor_copy(
-                    out=grouped[:].rearrange("p (t m j) -> p t m j", t=4, j=4)[:, :, m:gcut],
-                    in_=w1_raw[e, a][:].rearrange("p j (m t) -> p t m j", t=4)[:, :, m:gcut],
-                )
-            if gcut < 128:
-                nc.scalar.copy(out=dst[:, gcut:], in_=src[:, gcut:])
-            return grouped
+        w2_bf16 = aligned([P, E, N, PACK], BF16, "w2_bf16")
+        nc.vector.tensor_copy(
+            out=w2_bf16[:].rearrange("p e (c i) j -> p e c j i", i=4),
+            in_=w2_raw[:].rearrange("p e j (c i) -> p e c j i", i=4),
+        )
+        w2_codes = aligned([P, E, N], U32, "w2_codes")
+        w2_scales = aligned([P, E, N], U8, "w2_scales")
+        quantise(
+            w2_codes[:].rearrange("p e n -> p (e n)"),
+            w2_scales[:].rearrange("p e n -> p (e n)"),
+            w2_bf16[:].rearrange("p e n j -> p (e n j)"),
+        )
 
-        def quantise_w1(e, a, grouped):
-            codes = keep.tile([P, H], U32, name="w1_codes%d%d" % (e, a), align_bytes=64)
-            scales = keep.tile([P, H], U8, name="w1_scales%d%d" % (e, a), align_bytes=64)
-            nc.vector.quantize_mx(out=codes[:].bitcast(FP8X4), scales=scales[:], in_=grouped[:])
-            w1_codes[e, a] = codes
-            w1_scales[e, a] = scales
-
-        SHARES = {(0, 0): (0, 64), (0, 1): (0, 64), (1, 0): (0, 64), (1, 1): (0, 64), (2, 0): (0, 48), (2, 1): (64, 64), (3, 0): (64, 64), (3, 1): (128, 128)}
-        def prepare_w1(e, a):
-            quantise_w1(e, a, copy_w1(e, a, *SHARES.get((e, a), (0, 0))))
-
-        def prepare_w2():
-            w2_grouped = keep.tile([P, E, N, 4], BF16, name="w2_grouped", align_bytes=64)
-            nc.vector.tensor_copy(
-                out=w2_grouped[:].rearrange("p e (c i) j -> p e c j i", i=4),
-                in_=w2_raw[:].rearrange("p e j (c i) -> p e c j i", i=4),
-            )
-            w2_codes = keep.tile([P, E, N], U32, name="w2_codes", align_bytes=64)
-            w2_scales = keep.tile([P, E, N], U8, name="w2_scales", align_bytes=64)
-            nc.vector.quantize_mx(
-                out=w2_codes[:].rearrange("p e n -> p (e n)").bitcast(FP8X4),
-                scales=w2_scales[:].rearrange("p e n -> p (e n)"),
-                in_=w2_grouped[:].rearrange("p e n j -> p (e n j)"),
-            )
-            return w2_codes, w2_scales
-
-        y_sb = keep.tile([P, SLOTS], F32, name="y_sb")
-        H_TAGS = ["grouped21", "grouped30", "h2", "h3"]
-        h_grouped = {}
-        h_codes = [keep.tile([P, C], U32, name="h_codes%d" % e, align_bytes=64) for e in range(E)]
-        h_scales = [keep.tile([P, C], U8, name="h_scales%d" % e, align_bytes=64) for e in range(E)]
-        def layer1(e):
-            h_grouped[e] = keep.tile([P, C, 4], BF16, name="h_grouped%d" % e, tag=H_TAGS[e], align_bytes=64)
-            for c in range(C // CHUNK):
-                slots = slice(e * C + c * CHUNK, e * C + (c + 1) * CHUNK)
-                acc = sums.tile([P, 4, CHUNK], F32, name="acc")
-                for t in range(4):
+        h_codes = {}
+        h_scales = {}
+        for e in range(E):
+            h_bf16 = aligned([P, C, PACK], BF16, "h_bf16_%d" % e, H_BF16_AFTER.get(e))
+            h_codes[e] = aligned([P, C], U32, "h_codes%d" % e, H_CODES_AFTER.get(e))
+            h_scales[e] = aligned([P, C], U8, "h_scales%d" % e)
+            for lo in range(0, C, CHUNK):
+                slots = slice(e * C + lo, e * C + lo + CHUNK)
+                bank = hidden_banks.tile([P, PACK, CHUNK], F32, name="bank")
+                for t in range(PACK):
+                    units = slice(t * P, (t + 1) * P)
                     for a in range(PASSES):
                         nc.tensor.matmul_mx(
-                            out=acc[:, t, :],
-                            lhsT=w1_codes[e, a][:, t * P : (t + 1) * P].bitcast(FP8X4),
-                            lhsT_scale=w1_scales[e, a][:, t * P : (t + 1) * P],
-                            rhs=g_words[a][:, slots].bitcast(FP8X4),
-                            rhs_scale=g_bytes[a][:, slots],
+                            out=bank[:, t, :],
+                            lhsT=w1_codes[e, a][:, units].bitcast(FP8X4),
+                            lhsT_scale=w1_scales[e, a][:, units],
+                            rhs=slot_words[a][:, slots].bitcast(FP8X4),
+                            rhs_scale=slot_bytes[4 * a :, slots],
                             start=(a == 0),
                             stop=(a == PASSES - 1),
                         )
-                h_out = h_grouped[e][:, c * CHUNK : (c + 1) * CHUNK, :]
-                h_in = acc[:].rearrange("p t n -> p n t")
-                nc.scalar.activation(out=h_out, in_=h_in, func=RELU)
-            parts = 2 if e == E - 1 else 1
-            w = C // parts
-            for c in range(parts):
-                nc.vector.quantize_mx(
-                    out=h_codes[e][:, c * w : (c + 1) * w].bitcast(FP8X4),
-                    scales=h_scales[e][:, c * w : (c + 1) * w],
-                    in_=h_grouped[e][:, c * w : (c + 1) * w, :].rearrange("p n t -> p (n t)"),
+                nc.scalar.activation(
+                    out=h_bf16[:, lo : lo + CHUNK, :], in_=bank[:].rearrange("p t n -> p n t"), func=RELU
                 )
-        for e in range(3):
-            for a in range(PASSES):
-                prepare_w1(e, a)
-        layer1(0)
-        prepare_w1(3, 0)
-        layer1(1)
-        prepare_w1(3, 1)
-        layer1(2)
-        layer1(3)
-        w2_codes, w2_scales = prepare_w2()
+            step = CHUNK if e == E - 1 else C
+            for lo in range(0, C, step):
+                piece = slice(lo, lo + step)
+                quantise(h_codes[e][:, piece], h_scales[e][:, piece], h_bf16[:, piece, :].rearrange("p n t -> p (n t)"))
 
-        for e in range(E):
-            ysum = ysums.tile([P, C], F32, name="ysum")
+        y_sb = keep.tile([P, SLOTS], F32, name="y_sb")
+        y_first = y_banks.tile([P, 2 * C], F32, name="y_first")
+        y_third = y_banks.tile([P, C], F32, name="y_third")
+        y_fourth = [y_banks.tile([P, CHUNK], F32, name="y_fourth%d" % c) for c in range(2)]
+
+        def layer2(acc, e, lo, width):
             nc.tensor.matmul_mx(
-                out=ysum[:],
+                out=acc,
                 lhsT=w2_codes[:, e, :].bitcast(FP8X4),
                 lhsT_scale=w2_scales[:, e, :],
-                rhs=h_codes[e][:].bitcast(FP8X4),
-                rhs_scale=h_scales[e][:],
+                rhs=h_codes[e][:, lo : lo + width].bitcast(FP8X4),
+                rhs_scale=h_scales[e][:, lo : lo + width],
                 start=True,
                 stop=True,
             )
-            nc.scalar.copy(out=y_sb[:, e * C : (e + 1) * C], in_=ysum[:])
 
-        p1 = keep.tile([P, T], F32, name="p1")
-        p2 = keep.tile([P, T], F32, name="p2")
-        res = keep.tile([P, T], F32, name="res")
-        nc.vector.tensor_tensor(out=p1[:], in0=y_sb[:].indirect(pos1_sb[:]), in1=gate_sb[:, 0, :], op=MULT)
-        nc.vector.tensor_tensor(out=p2[:], in0=y_sb[:].indirect(pos2_sb[:]), in1=gate_sb[:, 1, :], op=MULT)
-        nc.vector.tensor_tensor(out=res[:], in0=p1[:], in1=p2[:], op=ADD)
-        nc.sync.dma_start(out=out, in_=res[:])
+        layer2(y_first[:, :C], 0, 0, C)
+        layer2(y_first[:, C:], 1, 0, C)
+        nc.scalar.copy(out=y_sb[:, : 2 * C], in_=y_first[:])
+        layer2(y_third[:], 2, 0, C)
+        nc.vector.tensor_copy(out=y_sb[:, 2 * C : 3 * C], in_=y_third[:])
+        for c in range(2):
+            layer2(y_fourth[c][:], 3, c * CHUNK, CHUNK)
+            nc.scalar.copy(out=y_sb[:, 3 * C + c * CHUNK : 3 * C + (c + 1) * CHUNK], in_=y_fourth[c][:])
+
+        first = keep.tile([P, T], F32, name="first")
+        second = keep.tile([P, T], F32, name="second")
+        result = keep.tile([P, T], F32, name="result")
+        nc.vector.tensor_tensor(out=first[:], in0=y_sb[:].indirect(pos1_sb[:]), in1=gate_sb[:, 0, :], op=MULT)
+        nc.vector.tensor_tensor(out=second[:], in0=y_sb[:].indirect(pos2_sb[:]), in1=gate_sb[:, 1, :], op=MULT)
+        nc.vector.tensor_tensor(out=result[:], in0=first[:], in1=second[:], op=ADD)
+        nc.sync.dma_start(out=out, in_=result[:])

@@ -105,7 +105,14 @@ def tile_routed_moe_kernel(tc, xT, w1, w2, gate, offs, pos1, pos2, out):
                     nc.scalar.copy(out=dst[:, cut:], in_=src[:, cut:])
                 w1_codes[e, a] = aligned([P, H], U32, "w1_codes%d%d" % (e, a))
                 w1_scales[e, a] = aligned([P, H], U8, "w1_scales%d%d" % (e, a))
-                quantise(w1_codes[e, a][:], w1_scales[e, a][:], w1_bf16[:])
+                pieces = 2 if (e, a) == (E - 1, PASSES - 1) else 1
+                step = H // pieces
+                for lo in range(0, H, step):
+                    quantise(
+                        w1_codes[e, a][:, lo : lo + step],
+                        w1_scales[e, a][:, lo : lo + step],
+                        w1_bf16[:, PACK * lo : PACK * (lo + step)],
+                    )
 
         w2_bf16 = aligned([P, E, N, PACK], BF16, "w2_bf16")
         nc.vector.tensor_copy(
@@ -170,9 +177,10 @@ def tile_routed_moe_kernel(tc, xT, w1, w2, gate, offs, pos1, pos2, out):
         nc.scalar.copy(out=y_sb[:, : 2 * C], in_=y_first[:])
         layer2(y_third[:], 2, 0, C)
         nc.vector.tensor_copy(out=y_sb[:, 2 * C : 3 * C], in_=y_third[:])
-        for c in range(2):
-            layer2(y_fourth[c][:], 3, c * CHUNK, CHUNK)
-            nc.scalar.copy(out=y_sb[:, 3 * C + c * CHUNK : 3 * C + (c + 1) * CHUNK], in_=y_fourth[c][:])
+        layer2(y_fourth[0][:], 3, 0, CHUNK)
+        nc.vector.tensor_copy(out=y_sb[:, 3 * C : 3 * C + CHUNK], in_=y_fourth[0][:])
+        layer2(y_fourth[1][:], 3, CHUNK, CHUNK)
+        nc.scalar.copy(out=y_sb[:, 3 * C + CHUNK :], in_=y_fourth[1][:])
 
         first = keep.tile([P, T], F32, name="first")
         second = keep.tile([P, T], F32, name="second")

from contextlib import ExitStack

import concourse.mybir as mybir

F32 = mybir.dt.float32
BF16 = mybir.dt.bfloat16
U32 = mybir.dt.uint32
U16 = mybir.dt.uint16
U8 = mybir.dt.uint8
FP8X4 = mybir.dt.float8_e4m3fn_x4
MULT = mybir.AluOpType.mult
ADD = mybir.AluOpType.add
RELU = mybir.ActivationFunctionType.Relu

K, T, E, C, H, N = 1024, 512, 4, 256, 512, 128
P = 128
PACK = 4
PASS = P * PACK
PASSES = K // PASS
SLOTS = E * C
CHUNK = 128
LIST_ROWS = 16

FLOPS = 2 * SLOTS * (K * H + H * N)

GATHER_CUTS = [(0, 384), (384, 768), (768, 1024)]

X_VECTOR_GROUPS = (88, 16)
W1_VECTOR_GROUPS = {(1, 0): 128, (2, 1): 128, (3, 0): 16, (3, 1): 48}

H_BF16_AFTER = {0: "w1_raw20", 1: "w1_raw31", 2: "w1_bf16_30"}
H_CODES_AFTER = {0: "w1_bf16_11", 1: "w1_bf16_20", 2: "w1_raw21"}


def tile_routed_moe_kernel(tc, xT, w1, w2, gate, offs, pos1, pos2, out):
    nc = tc.nc
    with ExitStack() as ctx:
        lists = ctx.enter_context(tc.tile_pool(name="lists", bufs=1))
        keep = ctx.enter_context(tc.tile_pool(name="keep", bufs=1))
        hidden_banks = ctx.enter_context(tc.psum_pool(name="hidden_banks", bufs=4))
        y_banks = ctx.enter_context(tc.psum_pool(name="y_banks", bufs=1))

        def aligned(shape, dtype, name, tag=None):
            return keep.tile(shape, dtype, name=name, tag=tag or name, align_bytes=64)

        def quantise(codes, scales, grouped):
            nc.vector.quantize_mx(out=codes.bitcast(FP8X4), scales=scales, in_=grouped)

        offs_sb = lists.tile([P, SLOTS // LIST_ROWS], U16, name="offs_sb")
        pos1_sb = lists.tile([P, T // LIST_ROWS], U16, name="pos1_sb")
        pos2_sb = lists.tile([P, T // LIST_ROWS], U16, name="pos2_sb")
        x_raw = [aligned([P, PACK, T], F32, "x_raw%d" % a) for a in range(PASSES)]
        w1_raw = {}
        for a in range(PASSES):
            rows = xT[PASS * a : PASS * (a + 1), :]
            nc.sync.dma_start(out=x_raw[a][:], in_=rows.rearrange("(p j) t -> p j t", j=PACK))
            if a == 0:
                nc.sync.dma_start(offs_sb[:], offs)
        for e in range(E):
            for a in range(PASSES):
                w1_raw[e, a] = aligned([P, PACK, H], F32, "w1_raw%d%d" % (e, a))
                rows = w1[e, PASS * a : PASS * (a + 1), :]
                nc.sync.dma_start(out=w1_raw[e, a][:], in_=rows.rearrange("(p j) i -> p j i", j=PACK))
        w2_raw = aligned([P, E, PACK, N], F32, "w2_raw")
        nc.sync.dma_start(
            out=w2_raw[:].rearrange("p e j n -> p e (j n)"),
            in_=w2.rearrange("e (p j) n -> p e (j n)", j=PACK),
        )
        nc.sync.dma_start(pos1_sb[:], pos1)
        nc.sync.dma_start(pos2_sb[:], pos2)
        gate_sb = keep.tile([P, 2, T], F32, name="gate_sb")
        nc.sync.dma_start(out=gate_sb[:], in_=gate.rearrange("r n t -> n r t"))

        x_bytes = aligned([P, T], U8, "x_bytes")
        nc.gpsimd.memset(x_bytes[:], 0)
        slot_words = [aligned([P, SLOTS], U32, "slot_words%d" % a) for a in range(PASSES)]
        slot_bytes = aligned([P, SLOTS], U8, "slot_bytes")
        for a in range(PASSES):
            x_bf16 = aligned([P, T, PACK], BF16, "x_bf16_%d" % a)
            dst = x_bf16[:].rearrange("p (c i) j -> p c j i", i=4)
            src = x_raw[a][:].rearrange("p j (c i) -> p c j i", i=4)
            cut = X_VECTOR_GROUPS[a]
            nc.vector.tensor_copy(out=dst[:, :cut], in_=src[:, :cut])
            nc.scalar.copy(out=dst[:, cut:], in_=src[:, cut:])
            x_words = aligned([P, T], U32, "x_words%d" % a)
            quantise(x_words[:], x_bytes[4 * a :, :], x_bf16[:].rearrange("p t j -> p (t j)"))
            for lo, hi in GATHER_CUTS:
                token_of_slot = offs_sb[:, lo // LIST_ROWS : hi // LIST_ROWS]
                nc.vector.tensor_copy(out=slot_words[a][:, lo:hi], in_=x_words[:].indirect(token_of_slot))
        for lo, hi in GATHER_CUTS:
            token_of_slot = offs_sb[:, lo // LIST_ROWS : hi // LIST_ROWS]
            nc.vector.tensor_copy(out=slot_bytes[:, lo:hi], in_=x_bytes[:].indirect(token_of_slot))

        w1_codes = {}
        w1_scales = {}
        for e in range(E):
            for a in range(PASSES):
                w1_bf16 = aligned([P, PACK * H], BF16, "w1_bf16_%d%d" % (e, a))
                dst = w1_bf16[:].rearrange("p (t m j) -> p m j t", t=4, j=PACK)
                src = w1_raw[e, a][:].rearrange("p j (m t) -> p m j t", t=4)
                cut = W1_VECTOR_GROUPS.get((e, a), 0)
                if cut > 0:
                    nc.vector.tensor_copy(out=dst[:, :cut], in_=src[:, :cut])
                if cut < H // 4:
                    nc.scalar.copy(out=dst[:, cut:], in_=src[:, cut:])
                w1_codes[e, a] = aligned([P, H], U32, "w1_codes%d%d" % (e, a))
                w1_scales[e, a] = aligned([P, H], U8, "w1_scales%d%d" % (e, a))
                pieces = 2 if (e, a) == (E - 1, PASSES - 1) else 1
                step = H // pieces
                for lo in range(0, H, step):
                    quantise(
                        w1_codes[e, a][:, lo : lo + step],
                        w1_scales[e, a][:, lo : lo + step],
                        w1_bf16[:, PACK * lo : PACK * (lo + step)],
                    )

        w2_bf16 = aligned([P, E, N, PACK], BF16, "w2_bf16")
        nc.vector.tensor_copy(
            out=w2_bf16[:].rearrange("p e (c i) j -> p e c j i", i=4),
            in_=w2_raw[:].rearrange("p e j (c i) -> p e c j i", i=4),
        )
        w2_codes = aligned([P, E, N], U32, "w2_codes")
        w2_scales = aligned([P, E, N], U8, "w2_scales")
        quantise(
            w2_codes[:].rearrange("p e n -> p (e n)"),
            w2_scales[:].rearrange("p e n -> p (e n)"),
            w2_bf16[:].rearrange("p e n j -> p (e n j)"),
        )

        h_codes = {}
        h_scales = {}
        for e in range(E):
            h_bf16 = aligned([P, C, PACK], BF16, "h_bf16_%d" % e, H_BF16_AFTER.get(e))
            h_codes[e] = aligned([P, C], U32, "h_codes%d" % e, H_CODES_AFTER.get(e))
            h_scales[e] = aligned([P, C], U8, "h_scales%d" % e)
            for lo in range(0, C, CHUNK):
                slots = slice(e * C + lo, e * C + lo + CHUNK)
                bank = hidden_banks.tile([P, PACK, CHUNK], F32, name="bank")
                for t in range(PACK):
                    units = slice(t * P, (t + 1) * P)
                    for a in range(PASSES):
                        nc.tensor.matmul_mx(
                            out=bank[:, t, :],
                            lhsT=w1_codes[e, a][:, units].bitcast(FP8X4),
                            lhsT_scale=w1_scales[e, a][:, units],
                            rhs=slot_words[a][:, slots].bitcast(FP8X4),
                            rhs_scale=slot_bytes[4 * a :, slots],
                            start=(a == 0),
                            stop=(a == PASSES - 1),
                        )
                nc.scalar.activation(
                    out=h_bf16[:, lo : lo + CHUNK, :], in_=bank[:].rearrange("p t n -> p n t"), func=RELU
                )
            step = CHUNK if e == E - 1 else C
            for lo in range(0, C, step):
                piece = slice(lo, lo + step)
                quantise(h_codes[e][:, piece], h_scales[e][:, piece], h_bf16[:, piece, :].rearrange("p n t -> p (n t)"))

        y_sb = keep.tile([P, SLOTS], F32, name="y_sb")
        y_first = y_banks.tile([P, 2 * C], F32, name="y_first")
        y_third = y_banks.tile([P, C], F32, name="y_third")
        y_fourth = [y_banks.tile([P, CHUNK], F32, name="y_fourth%d" % c) for c in range(2)]

        def layer2(acc, e, lo, width):
            nc.tensor.matmul_mx(
                out=acc,
                lhsT=w2_codes[:, e, :].bitcast(FP8X4),
                lhsT_scale=w2_scales[:, e, :],
                rhs=h_codes[e][:, lo : lo + width].bitcast(FP8X4),
                rhs_scale=h_scales[e][:, lo : lo + width],
                start=True,
                stop=True,
            )

        layer2(y_first[:, :C], 0, 0, C)
        layer2(y_first[:, C:], 1, 0, C)
        nc.scalar.copy(out=y_sb[:, : 2 * C], in_=y_first[:])
        layer2(y_third[:], 2, 0, C)
        nc.vector.tensor_copy(out=y_sb[:, 2 * C : 3 * C], in_=y_third[:])
        layer2(y_fourth[0][:], 3, 0, CHUNK)
        nc.vector.tensor_copy(out=y_sb[:, 3 * C : 3 * C + CHUNK], in_=y_fourth[0][:])
        layer2(y_fourth[1][:], 3, CHUNK, CHUNK)
        nc.scalar.copy(out=y_sb[:, 3 * C + CHUNK :], in_=y_fourth[1][:])

        first = keep.tile([P, T], F32, name="first")
        second = keep.tile([P, T], F32, name="second")
        result = keep.tile([P, T], F32, name="result")
        nc.vector.tensor_tensor(out=first[:], in0=y_sb[:].indirect(pos1_sb[:]), in1=gate_sb[:, 0, :], op=MULT)
        nc.vector.tensor_tensor(out=second[:], in0=y_sb[:].indirect(pos2_sb[:]), in1=gate_sb[:, 1, :], op=MULT)
        nc.vector.tensor_tensor(out=result[:], in0=first[:], in1=second[:], op=ADD)
        nc.sync.dma_start(out=out, in_=result[:])
